import numpy as np
import ml_dtypes


def mxq(x, axis, fmt="e4m3"):
    dtype, down = {"e4m3": (ml_dtypes.float8_e4m3fn, 7), "e5m2": (ml_dtypes.float8_e5m2, 14)}[fmt]
    v = np.moveaxis(np.asarray(x, np.float32).astype(ml_dtypes.bfloat16).astype(np.float64), axis, -1)
    blocks = v.reshape(v.shape[:-1] + (-1, 32))
    amax = np.abs(blocks).max(-1, keepdims=True)
    byte = np.maximum(np.where(amax > 0, np.frexp(amax)[1] - 1 + 127, 0) - down, 1)
    scale = np.exp2(byte - 127.0)
    codes = (blocks / scale).astype(np.float32).astype(dtype).astype(np.float64)
    return np.moveaxis((codes * scale).reshape(v.shape), -1, axis)


WIDE = False


def mx_kscale(k):
    if not WIDE:
        return np.ones(k)
    levels = np.array([10, -10, 5, -5, 0])
    if k % 512:
        return np.exp2(np.random.permutation(np.resize(levels, k // 32))).repeat(32)
    a = np.empty((k // 512, 16))
    for p in range(k // 512):
        a[p, :8] = np.random.permutation(np.resize(levels, 8))
        for g in range(8):
            far = levels[np.abs(levels - a[p, g]) >= 10]
            a[p, g + 8] = far[np.random.randint(len(far))]
    return np.exp2(a.ravel()).repeat(32)


def f64(x):
    return np.asarray(x).astype(np.float64)


def striped(idx):
    return np.tile(idx.reshape(-1, 16).T, (8, 1)).astype(np.uint16)


def unstriped(offs):
    return offs[:16].T.reshape(-1).astype(np.int64)


def pack_weight(w):
    k, n = w.shape
    w = f64(np.asarray(w, np.float32).astype(ml_dtypes.bfloat16)).reshape(k // 32, 32, n)
    amax = np.abs(w).max(1)
    byte = np.clip(np.where(amax > 0, np.frexp(amax)[1] - 1 + 127 - 7, 1), 1, 254)
    scaled = (w * np.exp2(127.0 - byte)[:, None, :]).reshape(k, n).astype(np.float32)
    words = np.ascontiguousarray(scaled.reshape(k // 512, 128, 4, n).transpose(0, 1, 3, 2)).astype(ml_dtypes.float8_e4m3fn).view(np.uint8)
    return words, np.ascontiguousarray(byte.astype(np.uint8).reshape(k // 512, 16, n))


def unpack_weight(words, scales):
    g, p, n, _ = words.shape
    vals = np.ascontiguousarray(words).view(ml_dtypes.float8_e4m3fn).astype(np.float64) * np.repeat(np.exp2(scales.astype(np.float64) - 127.0), 8, axis=1)[..., None]
    return vals.transpose(0, 1, 3, 2).reshape(g * 512, n)


def relu(v):
    return np.maximum(v, 0.0)


K, T, S, V, N = 512, 4096, 1536, 512, 256


def setup_inputs():
    n = np.random.standard_normal
    s = mx_kscale(K)[:, None]
    packed_xT = pack_weight(n((K, T)) * s)
    return {
        "x_words": packed_xT[0],
        "x_scales": packed_xT[1],
        "w1": (n((K, N)) / np.sqrt(K) / s).astype(np.float32),
        "w2": (n((K, N)) / np.sqrt(K) / s).astype(np.float32),
        "offs": striped(np.random.permutation(T)[:S]),
    }


def reference(x_words, x_scales, w1, w2, offs):
    xq = unpack_weight(x_words, x_scales)[:, unstriped(offs)]
    e = np.exp(mxq(f64(w1), 0, "e4m3").T @ xq)
    h = mxq(f64(w2), 0, "e4m3").T @ xq
    num = e[:, :V] * h[:, :V] + e[:, V:2 * V] * h[:, V:2 * V] + e[:, 2 * V:3 * V] * h[:, 2 * V:3 * V]
    den = e[:, :V] + e[:, V:2 * V] + e[:, 2 * V:3 * V]
    return relu(num / den)

@@ -1,0 +1,199 @@
+from contextlib import ExitStack
+
+import concourse.mybir as mybir
+from concourse.masks import make_identity
+
+K, T, S, V, N = 512, 4096, 1536, 512, 256
+FLOPS = 2 * 2 * K * S * N
+
+F32 = mybir.dt.float32
+BF16 = mybir.dt.bfloat16
+I32 = mybir.dt.int32
+U32 = mybir.dt.uint32
+U16 = mybir.dt.uint16
+U8 = mybir.dt.uint8
+FP8X4 = mybir.dt.float8_e4m3fn_x4
+ACT = mybir.ActivationFunctionType
+ALU = mybir.AluOpType
+
+P = 128
+PACK = 4
+PIECES = 3
+BLOCKS = V // P
+PAIRS = BLOCKS // 2
+BANK = 512
+LOG_CAP = 40.0
+
+
+def tile_picked_apool_relu_p_kernel(tc, x_words, x_scales, w1, w2, offs, out):
+    nc = tc.nc
+    with ExitStack() as ctx:
+        sb = ctx.enter_context(tc.tile_pool(name="sb", bufs=1))
+        ps = ctx.enter_context(tc.psum_pool(name="ps", bufs=1))
+
+        def bank(b):
+            return ps.tile([P, BANK], F32, name="bank%d" % b, tag="bank%d" % b)
+
+        offsets = sb.tile([P, S // 16], U16, name="offsets")
+        nc.sync.dma_start(offsets[:], offs)
+
+        scale_table = sb.tile([P, T], U8, name="scale_table", align_bytes=64)
+        for q in range(4):
+            rows = x_scales[0, 4 * q : 4 * q + 4, :].bitcast(I32)
+            nc.sync.dma_start(out=scale_table[32 * q : 32 * q + 32, :].bitcast(I32), in_=rows.partition_broadcast(8))
+
+        w1_raw = sb.tile([P, PACK, N], F32, name="w1_raw")
+        nc.sync.dma_start(out=w1_raw[:], in_=w1.rearrange("(p j) n -> p j n", j=PACK))
+        word_table = sb.tile([P, T], I32, name="word_table", align_bytes=64)
+        nc.sync.dma_start(out=word_table[:], in_=x_words[0].rearrange("p c r -> p (c r)").bitcast(I32))
+        w2_raw = sb.tile([P, PACK, N], F32, name="w2_raw")
+        nc.sync.dma_start(out=w2_raw[:], in_=w2.rearrange("(p j) n -> p j n", j=PACK))
+
+        ident = sb.tile([P, P], F32, name="ident")
+        make_identity(nc, ident[:])
+
+        w1_grouped = sb.tile([P, 2 * N, PACK], BF16, name="w1_grouped", align_bytes=64)
+        w1_k_last = w1_raw[:].rearrange("p j n -> p n j")
+        nc.scalar.activation(out=w1_grouped[:, 0:N, :], in_=w1_k_last, func=ACT.Copy)
+        nc.scalar.activation(out=w1_grouped[:, N : 2 * N, :], in_=w1_k_last, func=ACT.Copy, scale=-1.0)
+        w2_grouped = sb.tile([P, N, PACK], BF16, name="w2_grouped", align_bytes=64)
+        nc.scalar.activation(out=w2_grouped[:], in_=w2_raw[:].rearrange("p j n -> p n j"), func=ACT.Copy)
+
+        x_scale = sb.tile([P, S], U8, name="x_scale", align_bytes=64)
+        nc.vector.tensor_copy(x_scale[:], scale_table[:].indirect(offsets[:]))
+
+        w1_codes = sb.tile([P, 2 * N], U32, name="w1_codes", align_bytes=64)
+        w1_scale = sb.tile([P, 2 * N], U8, name="w1_scale", align_bytes=64)
+        nc.vector.quantize_mx(out=w1_codes[:].bitcast(FP8X4), scales=w1_scale[:], in_=w1_grouped[:].rearrange("p n j -> p (n j)"))
+
+        x_codes = []
+        for d in range(PIECES):
+            picked = sb.tile([P, V], U32, name="x_codes%d" % d, align_bytes=64)
+            piece = offsets[:, d * (V // 16) : (d + 1) * (V // 16)]
+            nc.vector.tensor_copy(picked[:], word_table[:].bitcast(U32).indirect(piece))
+            x_codes.append(picked)
+
+        w2_codes = sb.tile([P, N], U32, name="w2_codes", align_bytes=64)
+        w2_scale = sb.tile([P, N], U8, name="w2_scale", align_bytes=64)
+        nc.vector.quantize_mx(out=w2_codes[:].bitcast(FP8X4), scales=w2_scale[:], in_=w2_grouped[:].rearrange("p n j -> p (n j)"))
+
+        plus_w1 = (w1_codes[:, 0:N], w1_scale[:, 0:N])
+        minus_w1 = (w1_codes[:, N : 2 * N], w1_scale[:, N : 2 * N])
+        plus_w2 = (w2_codes[:], w2_scale[:])
+
+        def product(dst, d, block, weight, start, stop):
+            nc.tensor.matmul_mx(
+                out=dst,
+                lhsT=x_codes[d][:, block * P : (block + 1) * P].bitcast(FP8X4),
+                lhsT_scale=x_scale[:, d * V + block * P : d * V + (block + 1) * P],
+                rhs=weight[0].bitcast(FP8X4),
+                rhs_scale=weight[1],
+                start=start,
+                stop=stop,
+            )
+
+        def half(tile, i):
+            return tile[:, i * N : (i + 1) * N]
+
+        def score_gap(d, banks):
+            gaps = [bank(b) for b in banks]
+            for a in range(PAIRS):
+                for i in range(2):
+                    product(half(gaps[a], i), 0, 2 * a + i, minus_w1, i == 0, False)
+            for a in range(PAIRS):
+                for i in range(2):
+                    product(half(gaps[a], i), d, 2 * a + i, plus_w1, False, i == 1)
+            return gaps
+
+        gap1 = score_gap(1, (0, 1))
+        gap2 = score_gap(2, (6, 7))
+        h01 = []
+        for block in range(BLOCKS):
+            values = bank(2 + block)
+            for d in range(2):
+                product(half(values, d), d, block, plus_w2, True, True)
+            h01.append(values)
+
+        lift = [sb.tile([P, 2, N], F32, name="lift%d" % a) for a in range(PAIRS)]
+        e01 = [sb.tile([P, 2, 2, N], F32, name="e01_%d" % a) for a in range(PAIRS)]
+        log_e2 = sb.tile([P, BLOCKS * N], F32, name="log_e2")
+        e2 = sb.tile([P, BLOCKS * N], F32, name="e2")
+        for a in range(PAIRS):
+            nc.scalar.activation(out=lift[a][:].rearrange("p i n -> p (i n)"), in_=gap1[a][:], func=ACT.Relu)
+        for a in range(PAIRS):
+            nc.scalar.activation(out=e01[a][:, :, 1, :], in_=gap1[a][:].rearrange("p (i n) -> p i n", i=2), func=ACT.Exp)
+            nc.scalar.activation(out=e01[a][:, :, 0, :], in_=lift[a][:], func=ACT.Exp, scale=-1.0)
+        for a in range(PAIRS):
+            nc.vector.tensor_tensor(log_e2[:, a * BANK : (a + 1) * BANK], gap2[a][:], lift[a][:].rearrange("p i n -> p (i n)"), ALU.subtract)
+
+        h2 = []
+        for a in range(PAIRS):
+            values = bank(a)
+            for i in range(2):
+                product(half(values, i), 2, 2 * a + i, plus_w2, True, True)
+            h2.append(values)
+
+        eh01 = [sb.tile([P, 2, N], F32, name="eh01_%d" % b) for b in range(BLOCKS)]
+        eh2 = [sb.tile([P, 2, N], F32, name="eh2_%d" % a) for a in range(PAIRS)]
+
+        def weigh01(a):
+            for i in range(2):
+                block = 2 * a + i
+                nc.vector.tensor_tensor(
+                    eh01[block][:].rearrange("p d n -> p (d n)"), h01[block][:], e01[a][:, i, :, :].rearrange("p d n -> p (d n)"), ALU.mult
+                )
+
+        nc.vector.tensor_scalar_min(e01[0][:, :, 1, :], e01[0][:, :, 1, :], 1.0)
+        nc.vector.tensor_scalar_min(log_e2[:], log_e2[:], LOG_CAP)
+        nc.scalar.activation(out=e2[:], in_=log_e2[:], func=ACT.Exp)
+        weigh01(0)
+        nc.vector.tensor_scalar_min(e01[1][:, :, 1, :], e01[1][:, :, 1, :], 1.0)
+        weigh01(1)
+        for a in range(PAIRS):
+            nc.vector.tensor_tensor(eh2[a][:].rearrange("p i n -> p (i n)"), h2[a][:], e2[:, a * BANK : (a + 1) * BANK], ALU.mult)
+
+        def add_turned(total, source, d):
+            for i in range(2):
+                for f in range(2):
+                    col = f * 2 * P + i * P
+                    nc.tensor.matmul(
+                        out=total[:, col : col + P],
+                        lhsT=source(i)[:, f * P : (f + 1) * P],
+                        rhs=ident[:],
+                        is_transpose=True,
+                        start=(d == 0 and i == 0 and f == 0),
+                        stop=(d == PIECES - 1 and i == 1 and f == 1),
+                    )
+
+        den = [bank(6 + a) for a in range(PAIRS)]
+        num = [bank(2 + a) for a in range(PAIRS)]
+        for d in range(2):
+            add_turned(den[0], lambda i: e01[0][:, i, d, :], d)
+        for d in range(2):
+            add_turned(num[0], lambda i: eh01[i][:, d, :], d)
+        for d in range(2):
+            add_turned(den[1], lambda i: e01[1][:, i, d, :], d)
+        for a in range(PAIRS):
+            add_turned(den[a], lambda i: e2[:, (2 * a + i) * N : (2 * a + i + 1) * N], 2)
+        for d in range(2):
+            add_turned(num[1], lambda i: eh01[2 + i][:, d, :], d)
+        for a in range(PAIRS):
+            add_turned(num[a], lambda i: eh2[a][:, i, :], 2)
+
+        root = [sb.tile([P, BANK], F32, name="root%d" % a) for a in range(PAIRS)]
+        for a in range(PAIRS):
+            nc.scalar.activation(out=root[a][:], in_=den[a][:], func=ACT.Abs_reciprocal_sqrt)
+        inverse = sb.tile([P, BANK], F32, name="inverse")
+        nc.scalar.activation(out=inverse[:], in_=root[1][:], func=ACT.Square)
+
+        out_view = out.rearrange("(f p) v -> p f v", p=P)
+        once = sb.tile([P, BANK], F32, name="once")
+        result0 = sb.tile([P, 2, 2 * P], F32, name="result0")
+        nc.vector.scalar_tensor_tensor(once[:], num[0][:], 0.0, root[0][:], ALU.max, ALU.mult)
+        nc.vector.tensor_tensor(result0[:].rearrange("p f v -> p (f v)"), once[:], root[0][:], ALU.mult)
+        nc.sync.dma_start(out=out_view[:, :, 0 : 2 * P], in_=result0[:])
+        for f in range(2):
+            cols = slice(f * 2 * P, (f + 1) * 2 * P)
+            result1 = sb.tile([P, 2 * P], F32, name="result1_%d" % f)
+            nc.vector.scalar_tensor_tensor(result1[:], num[1][:, cols], 0.0, inverse[:, cols], ALU.max, ALU.mult)
+            nc.sync.dma_start(out=out_view[:, f, 2 * P : 4 * P], in_=result1[:])

@@ -22,7 +22,7 @@ PIECES = 3
 BLOCKS = V // P
 PAIRS = BLOCKS // 2
 BANK = 512
-LOG_CAP = 40.0
+CAP = 2.0**60
 
 
 def tile_picked_apool_relu_p_kernel(tc, x_words, x_scales, w1, w2, offs, out):
@@ -108,23 +108,32 @@ def tile_picked_apool_relu_p_kernel(tc, x_words, x_scales, w1, w2, offs, out):
         gap1 = score_gap(1, (0, 1))
         gap2 = score_gap(2, (6, 7))
         h01 = []
-        for block in range(BLOCKS):
-            values = bank(2 + block)
-            for d in range(2):
-                product(half(values, d), d, block, plus_w2, True, True)
+        for a in range(PAIRS):
+            values = [bank(2 + 2 * a + d) for d in range(2)]
+            for d in (1, 0):
+                for i in range(2):
+                    product(half(values[d], i), d, 2 * a + i, plus_w2, True, True)
             h01.append(values)
 
-        lift = [sb.tile([P, 2, N], F32, name="lift%d" % a) for a in range(PAIRS)]
-        e01 = [sb.tile([P, 2, 2, N], F32, name="e01_%d" % a) for a in range(PAIRS)]
-        log_e2 = sb.tile([P, BLOCKS * N], F32, name="log_e2")
-        e2 = sb.tile([P, BLOCKS * N], F32, name="e2")
+        def plane(name):
+            return [sb.tile([P, BANK], F32, name="%s%d" % (name, a)) for a in range(PAIRS)]
+
+        lift, tilt, tilt_abs, weight0, boost = plane("lift"), plane("tilt"), plane("tilt_abs"), plane("weight0"), plane("boost")
+        log_e2, e2, weight2 = plane("log_e2"), plane("e2"), plane("weight2")
+        terms = [plane("term%d_" % d) for d in range(PIECES)]
+
         for a in range(PAIRS):
-            nc.scalar.activation(out=lift[a][:].rearrange("p i n -> p (i n)"), in_=gap1[a][:], func=ACT.Relu)
+            nc.scalar.activation(out=lift[a][:], in_=gap1[a][:], func=ACT.Relu)
         for a in range(PAIRS):
-            nc.scalar.activation(out=e01[a][:, :, 1, :], in_=gap1[a][:].rearrange("p (i n) -> p i n", i=2), func=ACT.Exp)
-            nc.scalar.activation(out=e01[a][:, :, 0, :], in_=lift[a][:], func=ACT.Exp, scale=-1.0)
+            nc.scalar.activation(out=tilt[a][:], in_=gap1[a][:], func=ACT.Tanh, scale=0.5)
+            nc.gpsimd.tensor_scalar(weight0[a][:], tilt[a][:], -1.0, 1.0, ALU.mult, ALU.add)
         for a in range(PAIRS):
-            nc.vector.tensor_tensor(log_e2[:, a * BANK : (a + 1) * BANK], gap2[a][:], lift[a][:].rearrange("p i n -> p (i n)"), ALU.subtract)
+            nc.vector.tensor_tensor(log_e2[a][:], gap2[a][:], lift[a][:], ALU.subtract)
+        for a in range(PAIRS):
+            nc.scalar.activation(out=tilt_abs[a][:], in_=tilt[a][:], func=ACT.Abs)
+            nc.gpsimd.tensor_scalar(boost[a][:], tilt_abs[a][:], 1.0, 1.0, ALU.mult, ALU.add)
+        for a in range(PAIRS):
+            nc.scalar.activation(out=e2[a][:], in_=log_e2[a][:], func=ACT.Exp)
 
         h2 = []
         for a in range(PAIRS):
@@ -133,67 +142,56 @@ def tile_picked_apool_relu_p_kernel(tc, x_words, x_scales, w1, w2, offs, out):
                 product(half(values, i), 2, 2 * a + i, plus_w2, True, True)
             h2.append(values)
 
-        eh01 = [sb.tile([P, 2, N], F32, name="eh01_%d" % b) for b in range(BLOCKS)]
-        eh2 = [sb.tile([P, 2, N], F32, name="eh2_%d" % a) for a in range(PAIRS)]
-
-        def weigh01(a):
-            for i in range(2):
-                block = 2 * a + i
-                nc.vector.tensor_tensor(
-                    eh01[block][:].rearrange("p d n -> p (d n)"), h01[block][:], e01[a][:, i, :, :].rearrange("p d n -> p (d n)"), ALU.mult
-                )
-
-        nc.vector.tensor_scalar_min(e01[0][:, :, 1, :], e01[0][:, :, 1, :], 1.0)
-        nc.vector.tensor_scalar_min(log_e2[:], log_e2[:], LOG_CAP)
-        nc.scalar.activation(out=e2[:], in_=log_e2[:], func=ACT.Exp)
-        weigh01(0)
-        nc.vector.tensor_scalar_min(e01[1][:, :, 1, :], e01[1][:, :, 1, :], 1.0)
-        weigh01(1)
         for a in range(PAIRS):
-            nc.vector.tensor_tensor(eh2[a][:].rearrange("p i n -> p (i n)"), h2[a][:], e2[:, a * BANK : (a + 1) * BANK], ALU.mult)
+            nc.vector.scalar_tensor_tensor(terms[1][a][:], tilt[a][:], 1.0, h01[a][1][:], ALU.add, ALU.mult)
+            nc.vector.tensor_tensor(terms[0][a][:], h01[a][0][:], weight0[a][:], ALU.mult)
+        for a in range(PAIRS):
+            nc.vector.scalar_tensor_tensor(weight2[a][:], e2[a][:], CAP, boost[a][:], ALU.min, ALU.mult)
+        for a in range(PAIRS):
+            nc.vector.tensor_tensor(terms[2][a][:], h2[a][:], weight2[a][:], ALU.mult)
 
-        def add_turned(total, source, d):
+        def add_turned(total, source, first, last):
             for i in range(2):
                 for f in range(2):
                     col = f * 2 * P + i * P
                     nc.tensor.matmul(
                         out=total[:, col : col + P],
-                        lhsT=source(i)[:, f * P : (f + 1) * P],
+                        lhsT=source[:, i * N + f * P : i * N + (f + 1) * P],
                         rhs=ident[:],
                         is_transpose=True,
-                        start=(d == 0 and i == 0 and f == 0),
-                        stop=(d == PIECES - 1 and i == 1 and f == 1),
+                        start=(first and i == 0 and f == 0),
+                        stop=(last and i == 1 and f == 1),
                     )
 
         den = [bank(6 + a) for a in range(PAIRS)]
-        num = [bank(2 + a) for a in range(PAIRS)]
-        for d in range(2):
-            add_turned(den[0], lambda i: e01[0][:, i, d, :], d)
-        for d in range(2):
-            add_turned(num[0], lambda i: eh01[i][:, d, :], d)
-        for d in range(2):
-            add_turned(den[1], lambda i: e01[1][:, i, d, :], d)
+        num = [bank(3 + 2 * a) for a in range(PAIRS)]
         for a in range(PAIRS):
-            add_turned(den[a], lambda i: e2[:, (2 * a + i) * N : (2 * a + i + 1) * N], 2)
-        for d in range(2):
-            add_turned(num[1], lambda i: eh01[2 + i][:, d, :], d)
+            add_turned(num[a], terms[1][a], True, False)
+            add_turned(num[a], terms[0][a], False, False)
         for a in range(PAIRS):
-            add_turned(num[a], lambda i: eh2[a][:, i, :], 2)
-
-        root = [sb.tile([P, BANK], F32, name="root%d" % a) for a in range(PAIRS)]
+            add_turned(den[a], weight2[a], True, True)
         for a in range(PAIRS):
-            nc.scalar.activation(out=root[a][:], in_=den[a][:], func=ACT.Abs_reciprocal_sqrt)
-        inverse = sb.tile([P, BANK], F32, name="inverse")
-        nc.scalar.activation(out=inverse[:], in_=root[1][:], func=ACT.Square)
+            add_turned(num[a], terms[2][a], False, True)
 
         out_view = out.rearrange("(f p) v -> p f v", p=P)
-        once = sb.tile([P, BANK], F32, name="once")
-        result0 = sb.tile([P, 2, 2 * P], F32, name="result0")
-        nc.vector.scalar_tensor_tensor(once[:], num[0][:], 0.0, root[0][:], ALU.max, ALU.mult)
-        nc.vector.tensor_tensor(result0[:].rearrange("p f v -> p (f v)"), once[:], root[0][:], ALU.mult)
-        nc.sync.dma_start(out=out_view[:, :, 0 : 2 * P], in_=result0[:])
-        for f in range(2):
-            cols = slice(f * 2 * P, (f + 1) * 2 * P)
-            result1 = sb.tile([P, 2 * P], F32, name="result1_%d" % f)
-            nc.vector.scalar_tensor_tensor(result1[:], num[1][:, cols], 0.0, inverse[:, cols], ALU.max, ALU.mult)
-            nc.sync.dma_start(out=out_view[:, f, 2 * P : 4 * P], in_=result1[:])
+        quarters = [(a, f) for a in range(PAIRS) for f in range(2)]
+
+        def quarter(name):
+            return {q: sb.tile([P, 2 * P], F32, name="%s%d_%d" % (name, q[0], q[1])) for q in quarters}
+
+        def columns(tiles, q):
+            return tiles[q[0]][:, q[1] * 2 * P : (q[1] + 1) * 2 * P]
+
+        root, between, result = quarter("root"), quarter("between"), quarter("result")
+        for q in quarters:
+            nc.scalar.activation(out=root[q][:], in_=columns(den, q), func=ACT.Abs_reciprocal_sqrt, bias=2.0)
+        for q in quarters[2:]:
+            nc.scalar.activation(out=between[q][:], in_=root[q][:], func=ACT.Square)
+        for q in quarters[:2]:
+            nc.vector.scalar_tensor_tensor(between[q][:], columns(num, q), 0.0, root[q][:], ALU.max, ALU.mult)
+        for q in quarters[:2]:
+            nc.vector.tensor_tensor(result[q][:], between[q][:], root[q][:], ALU.mult)
+        for q in quarters[2:]:
+            nc.vector.scalar_tensor_tensor(result[q][:], columns(num, q), 0.0, between[q][:], ALU.max, ALU.mult)
+        for q in quarters:
+            nc.sync.dma_start(out=out_view[:, q[1], q[0] * 2 * P : (q[0] + 1) * 2 * P], in_=result[q][:])

@@ -37,13 +37,11 @@ def tile_picked_apool_relu_p_kernel(tc, x_words, x_scales, w1, w2, offs, out):
         offsets = sb.tile([P, S // 16], U16, name="offsets")
         nc.sync.dma_start(offsets[:], offs)
 
-        scale_table = sb.tile([P, T], U8, name="scale_table", align_bytes=64)
-        for q in range(4):
-            rows = x_scales[0, 4 * q : 4 * q + 4, :].bitcast(I32)
-            nc.sync.dma_start(out=scale_table[32 * q : 32 * q + 32, :].bitcast(I32), in_=rows.partition_broadcast(8))
-
-        w1_raw = sb.tile([P, PACK, N], F32, name="w1_raw")
+        w1_raw = sb.tile([P, PACK, N], F32, name="w1_raw", tag="early", align_bytes=64)
         nc.sync.dma_start(out=w1_raw[:], in_=w1.rearrange("(p j) n -> p j n", j=PACK))
+        scale_table = sb.tile([P, T], U8, name="scale_table", align_bytes=64)
+        nc.vector.memset(scale_table[:].bitcast(I32), 0)
+        nc.sync.dma_start(out=scale_table[0:P:8, :].bitcast(I32), in_=x_scales[0].bitcast(I32))
         word_table = sb.tile([P, T], I32, name="word_table", align_bytes=64)
         nc.sync.dma_start(out=word_table[:], in_=x_words[0].rearrange("p c r -> p (c r)").bitcast(I32))
         w2_raw = sb.tile([P, PACK, N], F32, name="w2_raw")
@@ -59,8 +57,12 @@ def tile_picked_apool_relu_p_kernel(tc, x_words, x_scales, w1, w2, offs, out):
         w2_grouped = sb.tile([P, N, PACK], BF16, name="w2_grouped", align_bytes=64)
         nc.scalar.activation(out=w2_grouped[:], in_=w2_raw[:].rearrange("p j n -> p n j"), func=ACT.Copy)
 
-        x_scale = sb.tile([P, S], U8, name="x_scale", align_bytes=64)
-        nc.vector.tensor_copy(x_scale[:], scale_table[:].indirect(offsets[:]))
+        picked_scale = sb.tile([P, S], U8, name="picked_scale", align_bytes=64)
+        nc.vector.tensor_copy(picked_scale[:], scale_table[:].indirect(offsets[:]))
+        x_scale = sb.tile([P, S], U8, name="x_scale", tag="early", align_bytes=64)
+        nc.vector.memset(x_scale[:].bitcast(I32), 0)
+        for i in range(4):
+            nc.scalar.dma_start(out=x_scale[i:P:32, :].bitcast(I32), in_=picked_scale[8 * i : P : 32, :].bitcast(I32))
 
         w1_codes = sb.tile([P, 2 * N], U32, name="w1_codes", align_bytes=64)
         w1_scale = sb.tile([P, 2 * N], U8, name="w1_scale", align_bytes=64)

@@ -36,8 +36,7 @@ def tile_picked_apool_relu_p_kernel(tc, x_words, x_scales, w1, w2, offs, out):
 
         offsets = sb.tile([P, S // 16], U16, name="offsets")
         nc.sync.dma_start(offsets[:], offs)
-
-        w1_raw = sb.tile([P, PACK, N], F32, name="w1_raw", tag="early", align_bytes=64)
+        w1_raw = sb.tile([P, PACK, N], F32, name="w1_raw")
         nc.sync.dma_start(out=w1_raw[:], in_=w1.rearrange("(p j) n -> p j n", j=PACK))
         scale_table = sb.tile([P, T], U8, name="scale_table", align_bytes=64)
         nc.vector.memset(scale_table[:].bitcast(I32), 0)
@@ -51,19 +50,24 @@ def tile_picked_apool_relu_p_kernel(tc, x_words, x_scales, w1, w2, offs, out):
         make_identity(nc, ident[:])
 
         w1_grouped = sb.tile([P, 2 * N, PACK], BF16, name="w1_grouped", align_bytes=64)
-        w1_k_last = w1_raw[:].rearrange("p j n -> p n j")
-        nc.scalar.activation(out=w1_grouped[:, 0:N, :], in_=w1_k_last, func=ACT.Copy)
-        nc.scalar.activation(out=w1_grouped[:, N : 2 * N, :], in_=w1_k_last, func=ACT.Copy, scale=-1.0)
+        nc.scalar.activation(out=w1_grouped[:, 0:N, :], in_=w1_raw[:].rearrange("p j n -> p n j"), func=ACT.Copy)
+
+        def scale_plane(first, count):
+            plane_tile = sb.tile([P, count], U8, name="x_scale%d" % first, align_bytes=64)
+            nc.vector.memset(plane_tile[:].bitcast(I32), 0)
+            picked = sb.tile([P, count], U8, name="picked_scale%d" % first, align_bytes=64)
+            nc.vector.tensor_copy(picked[:], scale_table[:].indirect(offsets[:, first // 16 : (first + count) // 16]))
+            for i in range(4):
+                nc.scalar.dma_start(out=plane_tile[i:P:32, :].bitcast(I32), in_=picked[8 * i : P : 32, :].bitcast(I32))
+            return plane_tile
+
+        scale_all = scale_plane(0, S)
+        x_scale = [scale_all[:, d * V : (d + 1) * V] for d in range(PIECES)]
+
         w2_grouped = sb.tile([P, N, PACK], BF16, name="w2_grouped", align_bytes=64)
         nc.scalar.activation(out=w2_grouped[:], in_=w2_raw[:].rearrange("p j n -> p n j"), func=ACT.Copy)
 
-        picked_scale = sb.tile([P, S], U8, name="picked_scale", align_bytes=64)
-        nc.vector.tensor_copy(picked_scale[:], scale_table[:].indirect(offsets[:]))
-        x_scale = sb.tile([P, S], U8, name="x_scale", tag="early", align_bytes=64)
-        nc.vector.memset(x_scale[:].bitcast(I32), 0)
-        for i in range(4):
-            nc.scalar.dma_start(out=x_scale[i:P:32, :].bitcast(I32), in_=picked_scale[8 * i : P : 32, :].bitcast(I32))
-
+        nc.vector.tensor_scalar_mul(w1_grouped[:, N : 2 * N, :], w1_grouped[:, 0:N, :], -1.0)
         w1_codes = sb.tile([P, 2 * N], U32, name="w1_codes", align_bytes=64)
         w1_scale = sb.tile([P, 2 * N], U8, name="w1_scale", align_bytes=64)
         nc.vector.quantize_mx(out=w1_codes[:].bitcast(FP8X4), scales=w1_scale[:], in_=w1_grouped[:].rearrange("p n j -> p (n j)"))
@@ -83,74 +87,29 @@ def tile_picked_apool_relu_p_kernel(tc, x_words, x_scales, w1, w2, offs, out):
         minus_w1 = (w1_codes[:, N : 2 * N], w1_scale[:, N : 2 * N])
         plus_w2 = (w2_codes[:], w2_scale[:])
 
-        def product(dst, d, block, weight, start, stop):
-            nc.tensor.matmul_mx(
-                out=dst,
-                lhsT=x_codes[d][:, block * P : (block + 1) * P].bitcast(FP8X4),
-                lhsT_scale=x_scale[:, d * V + block * P : d * V + (block + 1) * P],
-                rhs=weight[0].bitcast(FP8X4),
-                rhs_scale=weight[1],
-                start=start,
-                stop=stop,
-            )
-
-        def half(tile, i):
-            return tile[:, i * N : (i + 1) * N]
-
-        def score_gap(d, banks):
-            gaps = [bank(b) for b in banks]
-            for a in range(PAIRS):
-                for i in range(2):
-                    product(half(gaps[a], i), 0, 2 * a + i, minus_w1, i == 0, False)
-            for a in range(PAIRS):
-                for i in range(2):
-                    product(half(gaps[a], i), d, 2 * a + i, plus_w1, False, i == 1)
-            return gaps
-
-        gap1 = score_gap(1, (0, 1))
-        gap2 = score_gap(2, (6, 7))
-        h01 = []
-        for a in range(PAIRS):
-            values = [bank(2 + 2 * a + d) for d in range(2)]
-            for d in (1, 0):
-                for i in range(2):
-                    product(half(values[d], i), d, 2 * a + i, plus_w2, True, True)
-            h01.append(values)
-
-        def plane(name):
-            return [sb.tile([P, BANK], F32, name="%s%d" % (name, a)) for a in range(PAIRS)]
-
-        lift, tilt, tilt_abs, weight0, boost = plane("lift"), plane("tilt"), plane("tilt_abs"), plane("weight0"), plane("boost")
-        log_e2, e2, weight2 = plane("log_e2"), plane("e2"), plane("weight2")
-        terms = [plane("term%d_" % d) for d in range(PIECES)]
-
-        for a in range(PAIRS):
-            nc.scalar.activation(out=lift[a][:], in_=gap1[a][:], func=ACT.Relu)
-        for a in range(PAIRS):
-            nc.scalar.activation(out=tilt[a][:], in_=gap1[a][:], func=ACT.Tanh, scale=0.5)
-            nc.gpsimd.tensor_scalar(weight0[a][:], tilt[a][:], -1.0, 1.0, ALU.mult, ALU.add)
-        for a in range(PAIRS):
-            nc.vector.tensor_tensor(log_e2[a][:], gap2[a][:], lift[a][:], ALU.subtract)
-        for a in range(PAIRS):
-            nc.scalar.activation(out=tilt_abs[a][:], in_=tilt[a][:], func=ACT.Abs)
-            nc.gpsimd.tensor_scalar(boost[a][:], tilt_abs[a][:], 1.0, 1.0, ALU.mult, ALU.add)
-        for a in range(PAIRS):
-            nc.scalar.activation(out=e2[a][:], in_=log_e2[a][:], func=ACT.Exp)
-
-        h2 = []
-        for a in range(PAIRS):
-            values = bank(a)
+        def product(dst, d, a, weight, start, stop):
             for i in range(2):
-                product(half(values, i), 2, 2 * a + i, plus_w2, True, True)
-            h2.append(values)
+                places = slice((2 * a + i) * P, (2 * a + i + 1) * P)
+                nc.tensor.matmul_mx(
+                    out=dst[:, i * N : (i + 1) * N],
+                    lhsT=x_codes[d][:, places].bitcast(FP8X4),
+                    lhsT_scale=x_scale[d][:, places],
+                    rhs=weight[0].bitcast(FP8X4),
+                    rhs_scale=weight[1],
+                    start=(start and i == 0),
+                    stop=(stop and i == 1),
+                )
 
-        for a in range(PAIRS):
-            nc.vector.scalar_tensor_tensor(terms[1][a][:], tilt[a][:], 1.0, h01[a][1][:], ALU.add, ALU.mult)
-            nc.vector.tensor_tensor(terms[0][a][:], h01[a][0][:], weight0[a][:], ALU.mult)
-        for a in range(PAIRS):
-            nc.vector.scalar_tensor_tensor(weight2[a][:], e2[a][:], CAP, boost[a][:], ALU.min, ALU.mult)
-        for a in range(PAIRS):
-            nc.vector.tensor_tensor(terms[2][a][:], h2[a][:], weight2[a][:], ALU.mult)
+        def score_gap(b, d, a):
+            gap = bank(b)
+            product(gap, 0, a, minus_w1, True, False)
+            product(gap, d, a, plus_w1, False, True)
+            return gap
+
+        def values(b, d, a):
+            h = bank(b)
+            product(h, d, a, plus_w2, True, True)
+            return h
 
         def add_turned(total, source, first, last):
             for i in range(2):
@@ -165,15 +124,67 @@ def tile_picked_apool_relu_p_kernel(tc, x_words, x_scales, w1, w2, offs, out):
                         stop=(last and i == 1 and f == 1),
                     )
 
-        den = [bank(6 + a) for a in range(PAIRS)]
-        num = [bank(3 + 2 * a) for a in range(PAIRS)]
-        for a in range(PAIRS):
+        def plane(name):
+            return [sb.tile([P, BANK], F32, name="%s%d" % (name, a), tag="%s%d" % (name, a)) for a in range(PAIRS)]
+
+        lift, tilt, tilt_abs, weight0, boost = plane("lift"), plane("tilt"), plane("tilt_abs"), plane("weight0"), plane("boost")
+        log_e2, e2, weight2 = plane("log_e2"), plane("e2"), plane("weight2")
+        terms = [plane("term%d_" % d) for d in range(PIECES)]
+
+        gap1, gap2, h0, h1, h2, num, den = {}, {}, {}, {}, {}, {}, {}
+
+        def tilt_of(a):
+            nc.scalar.activation(out=lift[a][:], in_=gap1[a][:], func=ACT.Relu)
+            nc.scalar.activation(out=tilt[a][:], in_=gap1[a][:], func=ACT.Tanh, scale=0.5)
+            nc.gpsimd.tensor_scalar(weight0[a][:], tilt[a][:], -1.0, 1.0, ALU.mult, ALU.add)
+
+        def shift(a):
+            nc.vector.tensor_tensor(log_e2[a][:], gap2[a][:], lift[a][:], ALU.subtract)
+
+        def third(a):
+            nc.scalar.activation(out=tilt_abs[a][:], in_=tilt[a][:], func=ACT.Abs)
+            nc.gpsimd.tensor_scalar(boost[a][:], tilt_abs[a][:], 1.0, 1.0, ALU.mult, ALU.add)
+            nc.scalar.activation(out=e2[a][:], in_=log_e2[a][:], func=ACT.Exp)
+
+        def term1(a):
+            nc.vector.scalar_tensor_tensor(terms[1][a][:], tilt[a][:], 1.0, h1[a][:], ALU.add, ALU.mult)
+            num[a] = bank(3 + 2 * a)
             add_turned(num[a], terms[1][a], True, False)
+
+        def term0(a):
+            nc.vector.tensor_tensor(terms[0][a][:], h0[a][:], weight0[a][:], ALU.mult)
             add_turned(num[a], terms[0][a], False, False)
-        for a in range(PAIRS):
+
+        def denominator(a):
+            nc.vector.scalar_tensor_tensor(weight2[a][:], e2[a][:], CAP, boost[a][:], ALU.min, ALU.mult)
+            den[a] = bank(6 + a)
             add_turned(den[a], weight2[a], True, True)
-        for a in range(PAIRS):
+
+        def term2(a):
+            nc.vector.tensor_tensor(terms[2][a][:], h2[a][:], weight2[a][:], ALU.mult)
             add_turned(num[a], terms[2][a], False, True)
+
+        for a in range(PAIRS):
+            gap1[a] = score_gap(a, 1, a)
+            tilt_of(a)
+        for a in range(PAIRS):
+            gap2[a] = score_gap(6 + a, 2, a)
+            h1[a] = values(3 + 2 * a, 1, a)
+            h0[a] = values(2 + 2 * a, 0, a)
+        for a in range(PAIRS):
+            h2[a] = values(a, 2, a)
+        shift(0)
+        term1(0)
+        shift(1)
+        third(0)
+        third(1)
+        term0(0)
+        term1(1)
+        denominator(0)
+        term0(1)
+        denominator(1)
+        term2(0)
+        term2(1)
 
         out_view = out.rearrange("(f p) v -> p f v", p=P)
         quarters = [(a, f) for a in range(PAIRS) for f in range(2)]
@@ -185,15 +196,30 @@ def tile_picked_apool_relu_p_kernel(tc, x_words, x_scales, w1, w2, offs, out):
             return tiles[q[0]][:, q[1] * 2 * P : (q[1] + 1) * 2 * P]
 
         root, between, result = quarter("root"), quarter("between"), quarter("result")
-        for q in quarters:
-            nc.scalar.activation(out=root[q][:], in_=columns(den, q), func=ACT.Abs_reciprocal_sqrt, bias=2.0)
-        for q in quarters[2:]:
+
+        def roots(a):
+            for f in range(2):
+                nc.scalar.activation(out=root[a, f][:], in_=columns(den, (a, f)), func=ACT.Abs_reciprocal_sqrt, bias=2.0)
+
+        def square(q):
             nc.scalar.activation(out=between[q][:], in_=root[q][:], func=ACT.Square)
-        for q in quarters[:2]:
-            nc.vector.scalar_tensor_tensor(between[q][:], columns(num, q), 0.0, root[q][:], ALU.max, ALU.mult)
-        for q in quarters[:2]:
-            nc.vector.tensor_tensor(result[q][:], between[q][:], root[q][:], ALU.mult)
-        for q in quarters[2:]:
-            nc.vector.scalar_tensor_tensor(result[q][:], columns(num, q), 0.0, between[q][:], ALU.max, ALU.mult)
-        for q in quarters:
+
+        def scale(dst, q, factor):
+            nc.vector.scalar_tensor_tensor(dst[:], columns(num, q), 0.0, factor[:], ALU.max, ALU.mult)
+
+        def store(q):
             nc.sync.dma_start(out=out_view[:, q[1], q[0] * 2 * P : (q[0] + 1) * 2 * P], in_=result[q][:])
+
+        roots(0)
+        square((0, 0))
+        roots(1)
+        for f in range(2):
+            square((1, f))
+        scale(between[0, 1], (0, 1), root[0, 1])
+        scale(result[0, 0], (0, 0), between[0, 0])
+        store((0, 0))
+        nc.vector.tensor_tensor(result[0, 1][:], between[0, 1][:], root[0, 1][:], ALU.mult)
+        store((0, 1))
+        for f in range(2):
+            scale(result[1, f], (1, f), between[1, f])
+            store((1, f))

@@ -19,9 +19,13 @@ ALU = mybir.AluOpType
 P = 128
 PACK = 4
 PIECES = 3
-BLOCKS = V // P
-PAIRS = BLOCKS // 2
+HALVES = range(2)
+BLOCKS = range(2)
+FEATURE_TILES = range(2)
+HALF = 2 * P
 BANK = 512
+STRIPE = 16
+SCALE_STEP = 8
 CAP = 2.0**60
 
 
@@ -34,13 +38,17 @@ def tile_picked_apool_relu_p_kernel(tc, x_words, x_scales, w1, w2, offs, out):
         def bank(b):
             return ps.tile([P, BANK], F32, name="bank%d" % b, tag="bank%d" % b)
 
-        offsets = sb.tile([P, S // 16], U16, name="offsets")
+        offsets = sb.tile([P, S // STRIPE], U16, name="offsets")
         nc.sync.dma_start(offsets[:], offs)
+
         w1_raw = sb.tile([P, PACK, N], F32, name="w1_raw")
         nc.sync.dma_start(out=w1_raw[:], in_=w1.rearrange("(p j) n -> p j n", j=PACK))
+
         scale_table = sb.tile([P, T], U8, name="scale_table", align_bytes=64)
-        nc.vector.memset(scale_table[:].bitcast(I32), 0)
-        nc.sync.dma_start(out=scale_table[0:P:8, :].bitcast(I32), in_=x_scales[0].bitcast(I32))
+        nc.gpsimd.memset(scale_table[:, 0 : T // 2].bitcast(I32), 0)
+        nc.vector.memset(scale_table[:, T // 2 : T].bitcast(I32), 0)
+        nc.sync.dma_start(out=scale_table[0:P:SCALE_STEP, :].bitcast(I32), in_=x_scales[0].bitcast(I32))
+
         word_table = sb.tile([P, T], I32, name="word_table", align_bytes=64)
         nc.sync.dma_start(out=word_table[:], in_=x_words[0].rearrange("p c r -> p (c r)").bitcast(I32))
         w2_raw = sb.tile([P, PACK, N], F32, name="w2_raw")
@@ -49,23 +57,23 @@ def tile_picked_apool_relu_p_kernel(tc, x_words, x_scales, w1, w2, offs, out):
         ident = sb.tile([P, P], F32, name="ident")
         make_identity(nc, ident[:])
 
+        def interleave(grouped, raw):
+            nc.scalar.activation(
+                out=grouped.rearrange("p (c i) j -> p c j i", i=4), in_=raw[:].rearrange("p j (c i) -> p c j i", i=4), func=ACT.Copy
+            )
+
         w1_grouped = sb.tile([P, 2 * N, PACK], BF16, name="w1_grouped", align_bytes=64)
-        nc.scalar.activation(out=w1_grouped[:, 0:N, :], in_=w1_raw[:].rearrange("p j n -> p n j"), func=ACT.Copy)
+        interleave(w1_grouped[:, 0:N, :], w1_raw)
 
-        def scale_plane(first, count):
-            plane_tile = sb.tile([P, count], U8, name="x_scale%d" % first, align_bytes=64)
-            nc.vector.memset(plane_tile[:].bitcast(I32), 0)
-            picked = sb.tile([P, count], U8, name="picked_scale%d" % first, align_bytes=64)
-            nc.vector.tensor_copy(picked[:], scale_table[:].indirect(offsets[:, first // 16 : (first + count) // 16]))
-            for i in range(4):
-                nc.scalar.dma_start(out=plane_tile[i:P:32, :].bitcast(I32), in_=picked[8 * i : P : 32, :].bitcast(I32))
-            return plane_tile
-
-        scale_all = scale_plane(0, S)
-        x_scale = [scale_all[:, d * V : (d + 1) * V] for d in range(PIECES)]
+        x_scale = sb.tile([P, S], U8, name="x_scale", align_bytes=64)
+        nc.vector.memset(x_scale[:].bitcast(I32), 0)
+        picked_scale = sb.tile([P, S], U8, name="picked_scale", align_bytes=64)
+        nc.vector.tensor_copy(picked_scale[:], scale_table[:].indirect(offsets[:]))
+        for i in range(4):
+            nc.scalar.dma_start(out=x_scale[i:P:32, :].bitcast(I32), in_=picked_scale[SCALE_STEP * i : P : 32, :].bitcast(I32))
 
         w2_grouped = sb.tile([P, N, PACK], BF16, name="w2_grouped", align_bytes=64)
-        nc.scalar.activation(out=w2_grouped[:], in_=w2_raw[:].rearrange("p j n -> p n j"), func=ACT.Copy)
+        interleave(w2_grouped[:], w2_raw)
 
         nc.vector.tensor_scalar_mul(w1_grouped[:, N : 2 * N, :], w1_grouped[:, 0:N, :], -1.0)
         w1_codes = sb.tile([P, 2 * N], U32, name="w1_codes", align_bytes=64)
@@ -74,10 +82,10 @@ def tile_picked_apool_relu_p_kernel(tc, x_words, x_scales, w1, w2, offs, out):
 
         x_codes = []
         for d in range(PIECES):
-            picked = sb.tile([P, V], U32, name="x_codes%d" % d, align_bytes=64)
-            piece = offsets[:, d * (V // 16) : (d + 1) * (V // 16)]
-            nc.vector.tensor_copy(picked[:], word_table[:].bitcast(U32).indirect(piece))
-            x_codes.append(picked)
+            codes = sb.tile([P, V], U32, name="x_codes%d" % d, align_bytes=64)
+            piece = offsets[:, d * (V // STRIPE) : (d + 1) * (V // STRIPE)]
+            nc.vector.tensor_copy(codes[:], word_table[:].bitcast(U32).indirect(piece))
+            x_codes.append(codes)
 
         w2_codes = sb.tile([P, N], U32, name="w2_codes", align_bytes=64)
         w2_scale = sb.tile([P, N], U8, name="w2_scale", align_bytes=64)
@@ -88,23 +96,25 @@ def tile_picked_apool_relu_p_kernel(tc, x_words, x_scales, w1, w2, offs, out):
         plus_w2 = (w2_codes[:], w2_scale[:])
 
         def product(dst, d, a, weight, start, stop):
-            for i in range(2):
-                places = slice((2 * a + i) * P, (2 * a + i + 1) * P)
+            for i in BLOCKS:
+                first = a * HALF + i * P
                 nc.tensor.matmul_mx(
                     out=dst[:, i * N : (i + 1) * N],
-                    lhsT=x_codes[d][:, places].bitcast(FP8X4),
-                    lhsT_scale=x_scale[d][:, places],
+                    lhsT=x_codes[d][:, first : first + P].bitcast(FP8X4),
+                    lhsT_scale=x_scale[:, d * V + first : d * V + first + P],
                     rhs=weight[0].bitcast(FP8X4),
                     rhs_scale=weight[1],
-                    start=(start and i == 0),
-                    stop=(stop and i == 1),
+                    start=(start and i == BLOCKS[0]),
+                    stop=(stop and i == BLOCKS[-1]),
                 )
 
-        def score_gap(b, d, a):
+        def open_gap(b, a):
             gap = bank(b)
             product(gap, 0, a, minus_w1, True, False)
-            product(gap, d, a, plus_w1, False, True)
             return gap
+
+        def close_gap(gap, d, a):
+            product(gap, d, a, plus_w1, False, True)
 
         def values(b, d, a):
             h = bank(b)
@@ -112,26 +122,26 @@ def tile_picked_apool_relu_p_kernel(tc, x_words, x_scales, w1, w2, offs, out):
             return h
 
         def add_turned(total, source, first, last):
-            for i in range(2):
-                for f in range(2):
-                    col = f * 2 * P + i * P
+            for i in BLOCKS:
+                for f in FEATURE_TILES:
+                    col = f * HALF + i * P
                     nc.tensor.matmul(
                         out=total[:, col : col + P],
                         lhsT=source[:, i * N + f * P : i * N + (f + 1) * P],
                         rhs=ident[:],
                         is_transpose=True,
-                        start=(first and i == 0 and f == 0),
-                        stop=(last and i == 1 and f == 1),
+                        start=(first and i == BLOCKS[0] and f == FEATURE_TILES[0]),
+                        stop=(last and i == BLOCKS[-1] and f == FEATURE_TILES[-1]),
                     )
 
-        def plane(name):
-            return [sb.tile([P, BANK], F32, name="%s%d" % (name, a), tag="%s%d" % (name, a)) for a in range(PAIRS)]
+        def per_half(name):
+            return [sb.tile([P, BANK], F32, name="%s%d" % (name, a), tag="%s%d" % (name, a)) for a in HALVES]
 
-        lift, tilt, tilt_abs, weight0, boost = plane("lift"), plane("tilt"), plane("tilt_abs"), plane("weight0"), plane("boost")
-        log_e2, e2, weight2 = plane("log_e2"), plane("e2"), plane("weight2")
-        terms = [plane("term%d_" % d) for d in range(PIECES)]
+        lift, tilt, tilt_abs, weight0, boost = per_half("lift"), per_half("tilt"), per_half("tilt_abs"), per_half("weight0"), per_half("boost")
+        log_e2, e2, weight2 = per_half("log_e2"), per_half("e2"), per_half("weight2")
+        terms = [per_half("term%d_" % d) for d in range(PIECES)]
 
-        gap1, gap2, h0, h1, h2, num, den = {}, {}, {}, {}, {}, {}, {}
+        gap1, gap2, h0, h1, h2, num, weight2_turned = {}, {}, {}, {}, {}, {}, {}
 
         def tilt_of(a):
             nc.scalar.activation(out=lift[a][:], in_=gap1[a][:], func=ACT.Relu)
@@ -141,9 +151,11 @@ def tile_picked_apool_relu_p_kernel(tc, x_words, x_scales, w1, w2, offs, out):
         def shift(a):
             nc.vector.tensor_tensor(log_e2[a][:], gap2[a][:], lift[a][:], ALU.subtract)
 
-        def third(a):
+        def boost_of(a):
             nc.scalar.activation(out=tilt_abs[a][:], in_=tilt[a][:], func=ACT.Abs)
             nc.gpsimd.tensor_scalar(boost[a][:], tilt_abs[a][:], 1.0, 1.0, ALU.mult, ALU.add)
+
+        def exponential(a):
             nc.scalar.activation(out=e2[a][:], in_=log_e2[a][:], func=ACT.Exp)
 
         def term1(a):
@@ -155,71 +167,75 @@ def tile_picked_apool_relu_p_kernel(tc, x_words, x_scales, w1, w2, offs, out):
             nc.vector.tensor_tensor(terms[0][a][:], h0[a][:], weight0[a][:], ALU.mult)
             add_turned(num[a], terms[0][a], False, False)
 
-        def denominator(a):
+        def weight2_of(a):
             nc.vector.scalar_tensor_tensor(weight2[a][:], e2[a][:], CAP, boost[a][:], ALU.min, ALU.mult)
-            den[a] = bank(6 + a)
-            add_turned(den[a], weight2[a], True, True)
+            weight2_turned[a] = bank(6 + a)
+            add_turned(weight2_turned[a], weight2[a], True, True)
 
         def term2(a):
             nc.vector.tensor_tensor(terms[2][a][:], h2[a][:], weight2[a][:], ALU.mult)
             add_turned(num[a], terms[2][a], False, True)
 
-        for a in range(PAIRS):
-            gap1[a] = score_gap(a, 1, a)
+        for a in HALVES:
+            gap1[a] = open_gap(a, a)
+        for a in HALVES:
+            close_gap(gap1[a], 1, a)
             tilt_of(a)
-        for a in range(PAIRS):
-            gap2[a] = score_gap(6 + a, 2, a)
+        for a in HALVES:
+            gap2[a] = open_gap(6 + a, a)
+            close_gap(gap2[a], 2, a)
             h1[a] = values(3 + 2 * a, 1, a)
             h0[a] = values(2 + 2 * a, 0, a)
-        for a in range(PAIRS):
+        for a in HALVES:
             h2[a] = values(a, 2, a)
+
         shift(0)
         term1(0)
         shift(1)
-        third(0)
-        third(1)
+        for step in (boost_of, exponential):
+            for a in HALVES:
+                step(a)
         term0(0)
         term1(1)
-        denominator(0)
         term0(1)
-        denominator(1)
-        term2(0)
-        term2(1)
+        for step in (weight2_of, term2):
+            for a in HALVES:
+                step(a)
 
         out_view = out.rearrange("(f p) v -> p f v", p=P)
-        quarters = [(a, f) for a in range(PAIRS) for f in range(2)]
+        quarters = [(a, f) for a in HALVES for f in FEATURE_TILES]
 
-        def quarter(name):
-            return {q: sb.tile([P, 2 * P], F32, name="%s%d_%d" % (name, q[0], q[1])) for q in quarters}
+        def per_quarter(name):
+            return {q: sb.tile([P, HALF], F32, name="%s%d_%d" % (name, q[0], q[1])) for q in quarters}
 
-        def columns(tiles, q):
-            return tiles[q[0]][:, q[1] * 2 * P : (q[1] + 1) * 2 * P]
+        def columns(banks, q):
+            return banks[q[0]][:, q[1] * HALF : (q[1] + 1) * HALF]
 
-        root, between, result = quarter("root"), quarter("between"), quarter("result")
+        root, between, result = per_quarter("root"), per_quarter("between"), per_quarter("result")
 
         def roots(a):
-            for f in range(2):
-                nc.scalar.activation(out=root[a, f][:], in_=columns(den, (a, f)), func=ACT.Abs_reciprocal_sqrt, bias=2.0)
+            for f in FEATURE_TILES:
+                nc.scalar.activation(out=root[a, f][:], in_=columns(weight2_turned, (a, f)), func=ACT.Abs_reciprocal_sqrt, bias=2.0)
 
         def square(q):
             nc.scalar.activation(out=between[q][:], in_=root[q][:], func=ACT.Square)
 
-        def scale(dst, q, factor):
+        def relu_times(dst, q, factor):
             nc.vector.scalar_tensor_tensor(dst[:], columns(num, q), 0.0, factor[:], ALU.max, ALU.mult)
 
         def store(q):
-            nc.sync.dma_start(out=out_view[:, q[1], q[0] * 2 * P : (q[0] + 1) * 2 * P], in_=result[q][:])
+            nc.sync.dma_start(out=out_view[:, q[1], q[0] * HALF : (q[0] + 1) * HALF], in_=result[q][:])
 
         roots(0)
         square((0, 0))
         roots(1)
-        for f in range(2):
+        for f in FEATURE_TILES:
             square((1, f))
-        scale(between[0, 1], (0, 1), root[0, 1])
-        scale(result[0, 0], (0, 0), between[0, 0])
+        relu_times(between[0, 1], (0, 1), root[0, 1])
+        relu_times(result[0, 0], (0, 0), between[0, 0])
         store((0, 0))
         nc.vector.tensor_tensor(result[0, 1][:], between[0, 1][:], root[0, 1][:], ALU.mult)
         store((0, 1))
-        for f in range(2):
-            scale(result[1, f], (1, f), between[1, f])
+        for f in FEATURE_TILES:
+            relu_times(result[1, f], (1, f), between[1, f])
             store((1, f))

from contextlib import ExitStack

import concourse.mybir as mybir
from concourse.masks import make_identity

K, T, S, V, N = 512, 4096, 1536, 512, 256
FLOPS = 2 * 2 * K * S * N

F32 = mybir.dt.float32
BF16 = mybir.dt.bfloat16
I32 = mybir.dt.int32
U32 = mybir.dt.uint32
U16 = mybir.dt.uint16
U8 = mybir.dt.uint8
FP8X4 = mybir.dt.float8_e4m3fn_x4
ACT = mybir.ActivationFunctionType
ALU = mybir.AluOpType

P = 128
PACK = 4
PIECES = 3
HALVES = range(2)
BLOCKS = range(2)
FEATURE_TILES = range(2)
HALF = 2 * P
BANK = 512
STRIPE = 16
SCALE_STEP = 8
CAP = 2.0**60


def tile_picked_apool_relu_p_kernel(tc, x_words, x_scales, w1, w2, offs, out):
    nc = tc.nc
    with ExitStack() as ctx:
        sb = ctx.enter_context(tc.tile_pool(name="sb", bufs=1))
        ps = ctx.enter_context(tc.psum_pool(name="ps", bufs=1))

        def bank(b):
            return ps.tile([P, BANK], F32, name="bank%d" % b, tag="bank%d" % b)

        offsets = sb.tile([P, S // STRIPE], U16, name="offsets")
        nc.sync.dma_start(offsets[:], offs)

        w1_raw = sb.tile([P, PACK, N], F32, name="w1_raw")
        nc.sync.dma_start(out=w1_raw[:], in_=w1.rearrange("(p j) n -> p j n", j=PACK))

        scale_table = sb.tile([P, T], U8, name="scale_table", align_bytes=64)
        nc.gpsimd.memset(scale_table[:, 0 : T // 2].bitcast(I32), 0)
        nc.vector.memset(scale_table[:, T // 2 : T].bitcast(I32), 0)
        nc.sync.dma_start(out=scale_table[0:P:SCALE_STEP, :].bitcast(I32), in_=x_scales[0].bitcast(I32))

        word_table = sb.tile([P, T], I32, name="word_table", align_bytes=64)
        nc.sync.dma_start(out=word_table[:], in_=x_words[0].rearrange("p c r -> p (c r)").bitcast(I32))
        w2_raw = sb.tile([P, PACK, N], F32, name="w2_raw")
        nc.sync.dma_start(out=w2_raw[:], in_=w2.rearrange("(p j) n -> p j n", j=PACK))

        ident = sb.tile([P, P], F32, name="ident")
        make_identity(nc, ident[:])

        def interleave(grouped, raw):
            nc.scalar.activation(
                out=grouped.rearrange("p (c i) j -> p c j i", i=4), in_=raw[:].rearrange("p j (c i) -> p c j i", i=4), func=ACT.Copy
            )

        w1_grouped = sb.tile([P, 2 * N, PACK], BF16, name="w1_grouped", align_bytes=64)
        interleave(w1_grouped[:, 0:N, :], w1_raw)

        x_scale = sb.tile([P, S], U8, name="x_scale", align_bytes=64)
        nc.vector.memset(x_scale[:].bitcast(I32), 0)
        picked_scale = sb.tile([P, S], U8, name="picked_scale", align_bytes=64)
        nc.vector.tensor_copy(picked_scale[:], scale_table[:].indirect(offsets[:]))
        for i in range(4):
            nc.scalar.dma_start(out=x_scale[i:P:32, :].bitcast(I32), in_=picked_scale[SCALE_STEP * i : P : 32, :].bitcast(I32))

        w2_grouped = sb.tile([P, N, PACK], BF16, name="w2_grouped", align_bytes=64)
        interleave(w2_grouped[:], w2_raw)

        nc.vector.tensor_scalar_mul(w1_grouped[:, N : 2 * N, :], w1_grouped[:, 0:N, :], -1.0)
        w1_codes = sb.tile([P, 2 * N], U32, name="w1_codes", align_bytes=64)
        w1_scale = sb.tile([P, 2 * N], U8, name="w1_scale", align_bytes=64)
        nc.vector.quantize_mx(out=w1_codes[:].bitcast(FP8X4), scales=w1_scale[:], in_=w1_grouped[:].rearrange("p n j -> p (n j)"))

        x_codes = []
        for d in range(PIECES):
            codes = sb.tile([P, V], U32, name="x_codes%d" % d, align_bytes=64)
            piece = offsets[:, d * (V // STRIPE) : (d + 1) * (V // STRIPE)]
            nc.vector.tensor_copy(codes[:], word_table[:].bitcast(U32).indirect(piece))
            x_codes.append(codes)

        w2_codes = sb.tile([P, N], U32, name="w2_codes", align_bytes=64)
        w2_scale = sb.tile([P, N], U8, name="w2_scale", align_bytes=64)
        nc.vector.quantize_mx(out=w2_codes[:].bitcast(FP8X4), scales=w2_scale[:], in_=w2_grouped[:].rearrange("p n j -> p (n j)"))

        plus_w1 = (w1_codes[:, 0:N], w1_scale[:, 0:N])
        minus_w1 = (w1_codes[:, N : 2 * N], w1_scale[:, N : 2 * N])
        plus_w2 = (w2_codes[:], w2_scale[:])

        def product(dst, d, a, weight, start, stop):
            for i in BLOCKS:
                first = a * HALF + i * P
                nc.tensor.matmul_mx(
                    out=dst[:, i * N : (i + 1) * N],
                    lhsT=x_codes[d][:, first : first + P].bitcast(FP8X4),
                    lhsT_scale=x_scale[:, d * V + first : d * V + first + P],
                    rhs=weight[0].bitcast(FP8X4),
                    rhs_scale=weight[1],
                    start=(start and i == BLOCKS[0]),
                    stop=(stop and i == BLOCKS[-1]),
                )

        def open_gap(b, a):
            gap = bank(b)
            product(gap, 0, a, minus_w1, True, False)
            return gap

        def close_gap(gap, d, a):
            product(gap, d, a, plus_w1, False, True)

        def values(b, d, a):
            h = bank(b)
            product(h, d, a, plus_w2, True, True)
            return h

        def add_turned(total, source, first, last):
            for i in BLOCKS:
                for f in FEATURE_TILES:
                    col = f * HALF + i * P
                    nc.tensor.matmul(
                        out=total[:, col : col + P],
                        lhsT=source[:, i * N + f * P : i * N + (f + 1) * P],
                        rhs=ident[:],
                        is_transpose=True,
                        start=(first and i == BLOCKS[0] and f == FEATURE_TILES[0]),
                        stop=(last and i == BLOCKS[-1] and f == FEATURE_TILES[-1]),
                    )

        def per_half(name):
            return [sb.tile([P, BANK], F32, name="%s%d" % (name, a), tag="%s%d" % (name, a)) for a in HALVES]

        lift, tilt, tilt_abs, weight0, boost = per_half("lift"), per_half("tilt"), per_half("tilt_abs"), per_half("weight0"), per_half("boost")
        log_e2, e2, weight2 = per_half("log_e2"), per_half("e2"), per_half("weight2")
        terms = [per_half("term%d_" % d) for d in range(PIECES)]

        gap1, gap2, h0, h1, h2, num, weight2_turned = {}, {}, {}, {}, {}, {}, {}

        def tilt_of(a):
            nc.scalar.activation(out=lift[a][:], in_=gap1[a][:], func=ACT.Relu)
            nc.scalar.activation(out=tilt[a][:], in_=gap1[a][:], func=ACT.Tanh, scale=0.5)
            nc.gpsimd.tensor_scalar(weight0[a][:], tilt[a][:], -1.0, 1.0, ALU.mult, ALU.add)

        def shift(a):
            nc.vector.tensor_tensor(log_e2[a][:], gap2[a][:], lift[a][:], ALU.subtract)

        def boost_of(a):
            nc.scalar.activation(out=tilt_abs[a][:], in_=tilt[a][:], func=ACT.Abs)
            nc.gpsimd.tensor_scalar(boost[a][:], tilt_abs[a][:], 1.0, 1.0, ALU.mult, ALU.add)

        def exponential(a):
            nc.scalar.activation(out=e2[a][:], in_=log_e2[a][:], func=ACT.Exp)

        def term1(a):
            nc.vector.scalar_tensor_tensor(terms[1][a][:], tilt[a][:], 1.0, h1[a][:], ALU.add, ALU.mult)
            num[a] = bank(3 + 2 * a)
            add_turned(num[a], terms[1][a], True, False)

        def term0(a):
            nc.vector.tensor_tensor(terms[0][a][:], h0[a][:], weight0[a][:], ALU.mult)
            add_turned(num[a], terms[0][a], False, False)

        def weight2_of(a):
            nc.vector.scalar_tensor_tensor(weight2[a][:], e2[a][:], CAP, boost[a][:], ALU.min, ALU.mult)
            weight2_turned[a] = bank(6 + a)
            add_turned(weight2_turned[a], weight2[a], True, True)

        def term2(a):
            nc.vector.tensor_tensor(terms[2][a][:], h2[a][:], weight2[a][:], ALU.mult)
            add_turned(num[a], terms[2][a], False, True)

        for a in HALVES:
            gap1[a] = open_gap(a, a)
        for a in HALVES:
            close_gap(gap1[a], 1, a)
            tilt_of(a)
        for a in HALVES:
            gap2[a] = open_gap(6 + a, a)
            close_gap(gap2[a], 2, a)
            h1[a] = values(3 + 2 * a, 1, a)
            h0[a] = values(2 + 2 * a, 0, a)
        for a in HALVES:
            h2[a] = values(a, 2, a)

        shift(0)
        term1(0)
        shift(1)
        for step in (boost_of, exponential):
            for a in HALVES:
                step(a)
        term0(0)
        term1(1)
        term0(1)
        for step in (weight2_of, term2):
            for a in HALVES:
                step(a)

        out_view = out.rearrange("(f p) v -> p f v", p=P)
        quarters = [(a, f) for a in HALVES for f in FEATURE_TILES]

        def per_quarter(name):
            return {q: sb.tile([P, HALF], F32, name="%s%d_%d" % (name, q[0], q[1])) for q in quarters}

        def columns(banks, q):
            return banks[q[0]][:, q[1] * HALF : (q[1] + 1) * HALF]

        root, between, result = per_quarter("root"), per_quarter("between"), per_quarter("result")

        def roots(a):
            for f in FEATURE_TILES:
                nc.scalar.activation(out=root[a, f][:], in_=columns(weight2_turned, (a, f)), func=ACT.Abs_reciprocal_sqrt, bias=2.0)

        def square(q):
            nc.scalar.activation(out=between[q][:], in_=root[q][:], func=ACT.Square)

        def relu_times(dst, q, factor):
            nc.vector.scalar_tensor_tensor(dst[:], columns(num, q), 0.0, factor[:], ALU.max, ALU.mult)

        def store(q):
            nc.sync.dma_start(out=out_view[:, q[1], q[0] * HALF : (q[0] + 1) * HALF], in_=result[q][:])

        roots(0)
        square((0, 0))
        roots(1)
        for f in FEATURE_TILES:
            square((1, f))
        relu_times(between[0, 1], (0, 1), root[0, 1])
        relu_times(result[0, 0], (0, 0), between[0, 0])
        store((0, 0))
        nc.vector.tensor_tensor(result[0, 1][:], between[0, 1][:], root[0, 1][:], ALU.mult)
        store((0, 1))
        for f in FEATURE_TILES:
            relu_times(result[1, f], (1, f), between[1, f])
            store((1, f))
